import numpy as np
import ml_dtypes


def mxq(x, axis, fmt="e4m3"):
    dtype, down = {"e4m3": (ml_dtypes.float8_e4m3fn, 7), "e5m2": (ml_dtypes.float8_e5m2, 14)}[fmt]
    v = np.moveaxis(np.asarray(x, np.float32).astype(ml_dtypes.bfloat16).astype(np.float64), axis, -1)
    blocks = v.reshape(v.shape[:-1] + (-1, 32))
    amax = np.abs(blocks).max(-1, keepdims=True)
    byte = np.maximum(np.where(amax > 0, np.frexp(amax)[1] - 1 + 127, 0) - down, 1)
    scale = np.exp2(byte - 127.0)
    codes = (blocks / scale).astype(np.float32).astype(dtype).astype(np.float64)
    return np.moveaxis((codes * scale).reshape(v.shape), -1, axis)


WIDE = False


def mx_kscale(k):
    if not WIDE:
        return np.ones(k)
    levels = np.array([10, -10, 5, -5, 0])
    if k % 512:
        return np.exp2(np.random.permutation(np.resize(levels, k // 32))).repeat(32)
    a = np.empty((k // 512, 16))
    for p in range(k // 512):
        a[p, :8] = np.random.permutation(np.resize(levels, 8))
        for g in range(8):
            far = levels[np.abs(levels - a[p, g]) >= 10]
            a[p, g + 8] = far[np.random.randint(len(far))]
    return np.exp2(a.ravel()).repeat(32)


BF16 = ml_dtypes.bfloat16


def bf(x):
    return np.asarray(x, np.float32).astype(BF16)


def f64(x):
    return np.asarray(x).astype(np.float64)


E2M1 = np.array([0.0, 0.5, 1.0, 1.5, 2.0, 3.0, 4.0, 6.0, -0.0, -0.5, -1.0, -1.5, -2.0, -3.0, -4.0, -6.0])


def pack_weight(w, fmt):
    k, n = w.shape
    w = f64(bf(w)).reshape(k // 32, 32, n)
    amax = np.abs(w).max(1)
    if fmt == "e4m3":
        byte = np.frexp(amax)[1] - 1 + 127 - 7
    else:
        mant, ex = np.frexp(amax / 6.0)
        byte = np.where(mant > 0.5, ex, ex - 1) + 127
    byte = np.clip(np.where(amax > 0, byte, 1), 1, 254)
    scaled = (w * np.exp2(127.0 - byte)[:, None, :]).reshape(k, n).astype(np.float32)
    by_word = np.ascontiguousarray(scaled.reshape(k // 512, 128, 4, n).transpose(0, 1, 3, 2))
    if fmt == "e4m3":
        words = by_word.astype(ml_dtypes.float8_e4m3fn).view(np.uint8)
    else:
        c = by_word.astype(ml_dtypes.float4_e2m1fn).view(np.uint8) & 0xF
        words = c[..., 0::2] | (c[..., 1::2] << 4)
    return np.ascontiguousarray(words), np.ascontiguousarray(byte.astype(np.uint8).reshape(k // 512, 16, n))


def unpack_weight(words, scales, fmt):
    g, p, n, _ = words.shape
    if fmt == "e4m3":
        vals = np.ascontiguousarray(words).view(ml_dtypes.float8_e4m3fn).astype(np.float64)
    else:
        nib = np.empty((g, p, n, 4), np.uint8)
        nib[..., 0::2] = words & 0xF
        nib[..., 1::2] = words >> 4
        vals = E2M1[nib]
    vals = vals * np.repeat(np.exp2(scales.astype(np.float64) - 127.0), 8, axis=1)[..., None]
    return vals.transpose(0, 1, 3, 2).reshape(g * 512, n)
def pack4(w):
    words, scales = pack_weight(w, "e2m1")
    return words.reshape(words.shape[0], 128, -1), scales


def unpack4(words, scales):
    return unpack_weight(words.reshape(words.shape[0], 128, -1, 2), scales, "e2m1")


M, K, N, R = 1024, 1024, 2048, 512


def setup_inputs():
    s, u, t = mx_kscale(K), mx_kscale(K), mx_kscale(N)
    abn = np.random.standard_normal((K, M)) ** 4 / K
    sig = np.random.standard_normal((K, N)) ** 4 / 3.0
    abn_words, abn_scales = pack4(abn * s[:, None])
    sigq_words, sigq_scales = pack4(sig / s[:, None])
    gene_w = 0.5 + np.random.random_sample(N)
    counts = np.random.poisson(3.5, (M, N))
    return {"abn_words": abn_words, "abn_scales": abn_scales,
            "sigq_words": sigq_words, "sigq_scales": sigq_scales,
            "bg": bf(0.5 + 0.5 * np.random.random_sample(N)),
            "counts_w": bf(counts * gene_w * t),
            "gene_w": bf(gene_w * t),
            "sig": bf(sig * u[:, None] / t),
            "prog": bf(2.0 * np.random.standard_normal((K, R)) / np.sqrt(K * N) / u[:, None])}


def reference(abn_words, abn_scales, sigq_words, sigq_scales, bg, counts_w, gene_w, sig, prog):
    mu = unpack4(abn_words, abn_scales).T @ unpack4(sigq_words, sigq_scales)
    res = f64(counts_w) / (mu + f64(bg)) - f64(gene_w)
    proj = mxq(f64(sig), 0, "e4m3").T @ mxq(f64(prog), 0, "e4m3")
    return mxq(res, 1, "e4m3") @ mxq(proj, 0, "e4m3")

@@ -1,0 +1,516 @@
+from contextlib import ExitStack
+
+import concourse.mybir as mybir
+from concourse.masks import make_identity
+
+M, K, N, R = 1024, 1024, 2048, 512
+FLOPS = 2 * (M * N * K + N * R * K + M * R * N)
+
+F32 = mybir.dt.float32
+BF16 = mybir.dt.bfloat16
+I32 = mybir.dt.int32
+U32 = mybir.dt.uint32
+U8 = mybir.dt.uint8
+FP8X4 = mybir.dt.float8_e4m3fn_x4
+FP4X4 = mybir.dt.float4_e2m1fn_x4
+ACT = mybir.ActivationFunctionType
+ALU = mybir.AluOpType
+
+P = 128
+SLOTS = 4
+PASS = P * SLOTS
+K_PASSES = K // PASS
+GROUPS = N // PASS
+HALVES = M // PASS
+UNITS = HALVES * GROUPS
+PIECE = PASS // 2
+MU_BANKS = 3
+RECIP_BUFS = 4
+
+
+def tile_spatial_poisson_program_gradient_s12_kernel(
+    tc, abn_words, abn_scales, sigq_words, sigq_scales, bg, counts_w, gene_w, sig, prog, out
+):
+    nc = tc.nc
+
+    with ExitStack() as ctx:
+        keep = ctx.enter_context(tc.tile_pool(name="keep", bufs=1))
+        work = ctx.enter_context(tc.tile_pool(name="work", bufs=2))
+        psum = ctx.enter_context(tc.psum_pool(name="psum", bufs=1))
+        ctx.enter_context(tc.manual_schedule())
+
+        def kept(name, shape, dtype):
+            return keep.tile(shape, dtype, name=name, tag=name, align_bytes=64)
+
+        def rotating(tag, index, shape, dtype, bufs):
+            return work.tile(shape, dtype, name="%s_%d" % (tag, index), tag=tag, bufs=bufs, align_bytes=64)
+
+        def bank(tag, name, shape, dtype):
+            return psum.tile(shape, dtype, name=name, tag=tag)
+
+        def copy_on(engine, dst, src):
+            if engine == "vector":
+                nc.vector.tensor_copy(out=dst, in_=src)
+            elif engine == "gpsimd":
+                nc.gpsimd.tensor_scalar(out=dst, in0=src, scalar1=1.0, scalar2=0.0, op0=ALU.mult, op1=ALU.add)
+            else:
+                nc.scalar.copy(out=dst, in_=src)
+
+        a_scales = kept("a_scales", [P, K_PASSES * M], U8)
+        s_scales_raw = kept("s_scales_raw", [P, K_PASSES * N], U8)
+        s_scales = kept("s_scales", [P, SLOTS, K_PASSES * N // SLOTS], U8)
+        ident = kept("ident", [P, P], BF16)
+        bg_raw = kept("bg_raw", [GROUPS, PASS], BF16)
+        weight_raw = kept("weight_raw", [GROUPS, PASS], BF16)
+        bg_sorted = kept("bg_sorted", [P, PASS], BF16)
+        weight_sorted = kept("weight_sorted", [P, PASS], BF16)
+        bg_col = kept("bg_col", [P, SLOTS, GROUPS], F32)
+        warm = kept("warm", [P, 1], F32)
+        warm_out = kept("warm_out", [P, 1], F32)
+
+        nc.vector.memset(a_scales[:].bitcast(I32), 0)
+        nc.vector.memset(s_scales_raw[:].bitcast(I32), 0)
+        nc.vector.memset(warm[:], 1.0)
+        nc.vector.memset(bg_sorted[:], 0.0)
+        nc.vector.memset(weight_sorted[:], 0.0)
+        nc.scalar.activation(out=warm_out[:], in_=warm[:], func=ACT.Ln)
+
+        rows_raw = {}
+        counts_raw = {}
+        s_raw = {}
+        a_words = {}
+
+        def load_rows(key, rows):
+            raw = rotating("rows_raw", len(rows_raw), [P, SLOTS, PASS], BF16, 8)
+            nc.sync.dma_start(out=raw[:], in_=rows.rearrange("(p j) w -> p j w", j=SLOTS))
+            rows_raw[key] = raw
+
+        def load_prog(c):
+            load_rows(("prog", c), prog[c * PASS:(c + 1) * PASS, :])
+
+        def load_sig(g, c):
+            load_rows((g, c), sig[c * PASS:(c + 1) * PASS, g * PASS:(g + 1) * PASS])
+
+        def load_counts(u):
+            h, g = divmod(u, GROUPS)
+            raw = rotating("counts_raw", u, [P, SLOTS, PASS], BF16, 6)
+            rows = counts_w[h * PASS:(h + 1) * PASS, g * PASS:(g + 1) * PASS]
+            nc.sync.dma_start(out=raw[:], in_=rows.rearrange("(s p) n -> p s n", p=P))
+            counts_raw[u] = raw
+
+        def load_words(words, index, name):
+            raw = kept("%s_%d" % (name, index), [P, K_PASSES, 2 * PASS], U8)
+            part = words[:, :, index * 2 * PASS:(index + 1) * 2 * PASS].rearrange("c p n -> p c n")
+            nc.sync.dma_start(out=raw[:].bitcast(I32), in_=part.bitcast(I32))
+            return raw
+
+        def load_s(g):
+            s_raw[g] = load_words(sigq_words, g, "s_raw")
+
+        def load_a(h):
+            a_words[h] = load_words(abn_words, h, "a_words")
+
+        def load_scales(queue, plane, scales):
+            view = plane[:].rearrange("p (c n) -> p c n", c=K_PASSES)
+            for quad in range(4):
+                queue.dma_start(
+                    out=view[32 * quad:32 * quad + 4, :, :].bitcast(I32),
+                    in_=scales[:, 4 * quad:4 * quad + 4, :].rearrange("c r n -> r c n").bitcast(I32),
+                )
+
+        make_identity(nc, ident[:])
+        load_scales(nc.gpsimd, a_scales, abn_scales)
+        nc.gpsimd.dma_start(out=weight_raw[:], in_=gene_w.rearrange("(g n) -> g n", g=GROUPS))
+
+        load_s(0)
+        load_a(0)
+        nc.sync.dma_start(out=bg_raw[:], in_=bg.rearrange("(g n) -> g n", g=GROUPS))
+        load_prog(0)
+        load_scales(nc.sync, s_scales_raw, sigq_scales)
+        load_s(1)
+        load_prog(1)
+        load_counts(0)
+        load_sig(0, 0)
+        load_s(2)
+        load_sig(0, 1)
+        load_counts(1)
+        load_sig(1, 0)
+        load_s(3)
+        load_sig(1, 1)
+        load_counts(2)
+        load_a(1)
+        load_sig(2, 0)
+        load_counts(3)
+        load_sig(2, 1)
+        load_counts(4)
+        load_counts(5)
+
+        s_words = {}
+        grouped = {}
+        codes = {}
+        counts_sorted = {}
+        counts_t = {}
+        mu = {}
+        recip = {}
+        quot = {}
+        res_grouped = {}
+        proj_grouped = {}
+        proj_bank = {}
+        out_bank = {}
+
+        def sort_s(g):
+            dst = kept("s_words_%d" % g, [P, SLOTS, K_PASSES * 2 * P], U8)
+            src = s_raw[g][:].rearrange("p c n -> p (c n)").bitcast(I32)
+            nc.vector.tensor_copy(
+                out=dst[:].bitcast(I32).rearrange("p t (x w) -> p t x w", w=4),
+                in_=src.rearrange("p (x t w) -> p t x w", t=SLOTS, w=4),
+            )
+            s_words[g] = dst
+
+        def sort_s_scales():
+            nc.vector.tensor_copy(
+                out=s_scales[:].bitcast(I32).rearrange("p t (x w) -> p t x w", w=2),
+                in_=s_scales_raw[:].bitcast(I32).rearrange("p (x t w) -> p t x w", t=SLOTS, w=2),
+            )
+
+        def interleave_prog(c, engine):
+            key = ("prog", c)
+            dst = rotating("grouped", len(grouped), [P, PASS * SLOTS], BF16, 2)
+            copy_on(
+                engine,
+                dst[:].rearrange("p (x i j) -> p x j i", i=4, j=SLOTS),
+                rows_raw[key][:].rearrange("p j (x i) -> p x j i", i=4),
+            )
+            grouped[key] = dst
+
+        def interleave_sig(g, c, engine, gate=False):
+            key = (g, c)
+            if gate:
+                dst = rotating("grouped_gpsimd", len(grouped), [P, PASS * SLOTS], BF16, 1)
+            else:
+                dst = rotating("grouped", len(grouped), [P, PASS * SLOTS], BF16, 2)
+            dst_view = dst[:].rearrange("p (t q a i j) -> p a q t j i", t=SLOTS, a=2, i=4, j=SLOTS)
+            src_view = rows_raw[key][:].rearrange("p j (q t a i) -> p a q t j i", t=SLOTS, a=2, i=4)
+            if engine == "gpsimd":
+                nc.gpsimd.tensor_scalar(
+                    out=dst[:].rearrange("p (t q r j) -> p q t r j", t=SLOTS, r=8, j=SLOTS),
+                    in0=rows_raw[key][:].rearrange("p j (q t r) -> p q t r j", t=SLOTS, r=8),
+                    scalar1=1.0, scalar2=0.0, op0=ALU.mult, op1=ALU.add,
+                )
+            else:
+                for a in range(2):
+                    copy_on(engine, dst_view[:, a], src_view[:, a])
+            grouped[key] = dst
+
+        def code_tiles(key):
+            if key not in codes:
+                name = "_".join(str(part) for part in key)
+                codes[key] = (kept("codes_" + name, [P, PASS], U32), kept("scales_" + name, [P, PASS], U8))
+            return codes[key]
+
+        def quantize(key, src, start=0, stop=PASS):
+            words, scales = code_tiles(key)
+            nc.vector.quantize_mx(
+                out=words[:, start:stop].bitcast(FP8X4),
+                scales=scales[:, start:stop],
+                in_=src[:, start * SLOTS:stop * SLOTS],
+            )
+
+        def quantize_rows(key):
+            quantize(key, grouped[key])
+
+        def sort_counts(u, engine, gate=False):
+            if gate:
+                dst = rotating("grouped_gpsimd", 100 + u, [P, SLOTS, PASS], BF16, 1)
+            else:
+                dst = rotating("counts_sorted", u, [P, SLOTS, PASS], BF16, 2)
+            src = counts_raw[u][:].rearrange("p s n -> p (s n)")
+            copy_on(
+                engine,
+                dst[:].rearrange("p t (x r) -> p t x r", r=8),
+                src.rearrange("p (x t r) -> p t x r", t=SLOTS, r=8),
+            )
+            counts_sorted[u] = dst
+
+        def transpose_counts(u):
+            for piece in range(2):
+                dst = bank("counts_t%d" % piece, "counts_t_%d_%d" % (u, piece), [P, SLOTS, PIECE], BF16)
+                for t in range(SLOTS):
+                    for s in range(2):
+                        col = piece * PIECE + s * P
+                        nc.tensor.transpose(dst[:, t, s * P:(s + 1) * P], counts_sorted[u][:, t, col:col + P], ident[:])
+                counts_t[(u, piece)] = dst
+
+        def mu_matmul(n):
+            if n >= UNITS * SLOTS:
+                return
+            u, t = divmod(n, SLOTS)
+            h, g = divmod(u, GROUPS)
+            dst = bank("mu%d" % (n % MU_BANKS), "mu_%d" % n, [P, PASS], F32)
+            for c in range(K_PASSES):
+                s_col = (c * GROUPS + g) * P
+                a_col = c * M + h * PASS
+                nc.tensor.matmul_mx(
+                    out=dst[:],
+                    lhsT=s_words[g][:, t, c * 2 * P:(c + 1) * 2 * P].bitcast(FP4X4),
+                    lhsT_scale=s_scales[:, t, s_col:s_col + P],
+                    rhs=a_words[h][:, c, :].bitcast(FP4X4),
+                    rhs_scale=a_scales[:, a_col:a_col + PASS],
+                    start=(c == 0),
+                    stop=(c == K_PASSES - 1),
+                )
+            mu[n] = dst
+
+        def log_rate(u, ahead=SLOTS):
+            g = u % GROUPS
+            dst = rotating("recip", u, [P, SLOTS, PASS], F32, RECIP_BUFS)
+            recip[u] = dst
+            for t in range(SLOTS):
+                n = u * SLOTS + t
+                nc.scalar.activation(out=dst[:, t, :], in_=mu[n][:], func=ACT.Ln, bias=bg_col[:, t, g:g + 1])
+                if t < ahead:
+                    mu_matmul(n + MU_BANKS)
+
+        def inverse_rate(u):
+            for piece in range(2):
+                part = recip[u][:, :, piece * PIECE:(piece + 1) * PIECE]
+                nc.scalar.activation(out=part, in_=part, func=ACT.Exp, scale=-1.0)
+
+        def multiply(u, piece):
+            dst = rotating("quot", 2 * u + piece, [P, SLOTS, PIECE], F32, 2)
+            nc.vector.tensor_tensor(
+                out=dst[:], in0=counts_t[(u, piece)][:], in1=recip[u][:, :, piece * PIECE:(piece + 1) * PIECE], op=ALU.mult
+            )
+            quot[(u, piece)] = dst
+
+        def subtract(u, piece):
+            g = u % GROUPS
+            if piece == 0:
+                res_grouped[u] = rotating("res_grouped", u, [P, PASS * SLOTS], BF16, 2)
+            part = res_grouped[u][:, piece * PIECE * SLOTS:(piece + 1) * PIECE * SLOTS]
+            weights = weight_t[:, :, g:g + 1].rearrange("p t (x i) -> p x t i", x=1)
+            nc.vector.tensor_tensor(
+                out=part.rearrange("p (x i t) -> p x t i", i=2, t=SLOTS),
+                in0=quot[(u, piece)][:].rearrange("p t (x i) -> p x t i", i=2),
+                in1=weights.to_broadcast([P, PIECE // 2, SLOTS, 2]),
+                op=ALU.subtract,
+            )
+
+        proj_tags = {(2, 2): "mu2", (2, 3): "mu0", (3, 2): "mu1", (3, 3): "mu2"}
+
+        def proj_matmul(g, b):
+            dst = bank(proj_tags.get((g, b), "acc%d" % (b % 2)), "proj_%d_%d" % (g, b), [P, SLOTS, P], F32)
+            cols = slice(b * P, (b + 1) * P)
+            for t in range(SLOTS):
+                genes = slice(t * P, (t + 1) * P)
+                for c in range(K_PASSES):
+                    nc.tensor.matmul_mx(
+                        out=dst[:, t, :],
+                        lhsT=codes[(g, c)][0][:, genes].bitcast(FP8X4),
+                        lhsT_scale=codes[(g, c)][1][:, genes],
+                        rhs=codes[("prog", c)][0][:, cols].bitcast(FP8X4),
+                        rhs_scale=codes[("prog", c)][1][:, cols],
+                        start=(c == 0),
+                        stop=(c == K_PASSES - 1),
+                    )
+            proj_bank[(g, b)] = dst
+
+        def proj_copy(g, b, engine):
+            if b == 0:
+                proj_grouped[g] = rotating("proj_grouped", g, [P, R * SLOTS], BF16, 2)
+            part = proj_grouped[g][:, b * P * SLOTS:(b + 1) * P * SLOTS]
+            copy_on(engine, part.rearrange("p (r t) -> p r t", t=SLOTS), proj_bank[(g, b)][:].rearrange("p t r -> p r t"))
+
+        out_tags = ["mu0", "acc0", "acc1", "mu1", "mu2", "mu0", "acc0", "acc1"]
+
+        def out_matmul(m, g):
+            h, s = divmod(m, SLOTS)
+            if g == 0:
+                out_bank[m] = bank(out_tags[m], "out_%d" % m, [P, R], F32)
+            spots = slice(s * P, (s + 1) * P)
+            words, scales = codes[("res", h * GROUPS + g)]
+            nc.tensor.matmul_mx(
+                out=out_bank[m][:],
+                lhsT=words[:, spots].bitcast(FP8X4),
+                lhsT_scale=scales[:, spots],
+                rhs=codes[("proj", g)][0][:].bitcast(FP8X4),
+                rhs_scale=codes[("proj", g)][1][:],
+                start=(g == 0),
+                stop=(g == GROUPS - 1),
+            )
+
+        def out_store(m, engine):
+            result = rotating("result", m, [P, R], F32, 4)
+            copy_on(engine, result[:], out_bank[m][:])
+            nc.sync.dma_start(out=out[m * P:(m + 1) * P, :], in_=result[:])
+
+        V, S, G = "vector", "scalar", "gpsimd"
+
+        def unit(u):
+            multiply(u, 0)
+            multiply(u, 1)
+            subtract(u, 0)
+            subtract(u, 1)
+
+        def proj_pair(g, b, engine):
+            proj_copy(g, b, engine)
+            proj_copy(g, b + 1, engine)
+
+        def proj_mm(g, b):
+            proj_matmul(g, b)
+            proj_matmul(g, b + 1)
+
+        def q_res(u):
+            quantize(("res", u), res_grouped[u])
+
+        def q_proj(g):
+            quantize(("proj", g), proj_grouped[g])
+
+        def vector_columns(raw, sorted_rows, tag):
+            nc.scalar.copy(
+                out=sorted_rows[:GROUPS, :].rearrange("p (t q r) -> p t q r", t=SLOTS, r=8),
+                in_=raw[:].rearrange("p (q t r) -> p t q r", t=SLOTS, r=8),
+            )
+            dst = bank(tag, "columns_" + tag, [P, SLOTS, P], BF16)
+            for t in range(SLOTS):
+                nc.tensor.transpose(dst[:, t, :], sorted_rows[:, t * P:(t + 1) * P], ident[:])
+            return dst
+
+        bg_t = vector_columns(bg_raw, bg_sorted, "acc0")
+        nc.scalar.copy(out=bg_col[:], in_=bg_t[:, :, :GROUPS])
+        sort_s(0)
+        interleave_prog(0, V)
+        sort_s_scales()
+        for n in range(MU_BANKS):
+            mu_matmul(n)
+        quantize_rows(("prog", 0))
+        sort_s(1)
+        log_rate(0)
+        interleave_prog(1, V)
+        load_sig(3, 0)
+        load_sig(3, 1)
+        sort_counts(0, V)
+        load_counts(6)
+        quantize_rows(("prog", 1))
+        interleave_sig(0, 0, V)
+        log_rate(1, 1)
+        weight_t = vector_columns(weight_raw, weight_sorted, "weights")
+        transpose_counts(0)
+        sort_s(2)
+        mu_matmul(8)
+        mu_matmul(9)
+        mu_matmul(10)
+        quantize_rows((0, 0))
+        interleave_sig(0, 1, V, True)
+        sort_counts(1, V)
+        load_counts(7)
+        sort_s(3)
+        quantize_rows((0, 1))
+        inverse_rate(0)
+        inverse_rate(1)
+        proj_mm(0, 0)
+        interleave_sig(1, 0, G, True)
+        interleave_sig(1, 1, G)
+        multiply(0, 0)
+        multiply(0, 1)
+        transpose_counts(1)
+        proj_pair(0, 0, V)
+        proj_mm(0, 2)
+        subtract(0, 0)
+        subtract(0, 1)
+        proj_pair(0, 2, V)
+        log_rate(2)
+        sort_counts(2, V)
+        q_res(0)
+        quantize_rows((1, 1))
+        quantize_rows((1, 0))
+        interleave_sig(2, 0, G, True)
+        log_rate(3)
+        unit(1)
+        log_rate(4)
+        transpose_counts(2)
+        proj_mm(1, 0)
+        q_proj(0)
+        q_res(1)
+        sort_counts(3, V)
+        quantize_rows((2, 0))
+        inverse_rate(2)
+        interleave_sig(2, 1, G, True)
+        unit(2)
+        transpose_counts(3)
+        proj_pair(1, 0, S)
+        proj_mm(1, 2)
+        inverse_rate(3)
+        proj_pair(1, 2, S)
+        inverse_rate(4)
+        sort_counts(4, V)
+        q_res(2)
+        quantize_rows((2, 1))
+        proj_mm(2, 0)
+        interleave_sig(3, 0, G, True)
+        unit(3)
+        transpose_counts(4)
+        log_rate(5)
+        log_rate(6)
+        sort_counts(5, V)
+        q_proj(1)
+        q_res(3)
+        quantize_rows((3, 0))
+        interleave_sig(3, 1, G, True)
+        unit(4)
+        log_rate(7)
+        transpose_counts(5)
+        proj_mm(2, 2)
+        inverse_rate(5)
+        proj_pair(2, 0, S)
+        sort_counts(6, V)
+        q_res(4)
+        quantize_rows((3, 1))
+        proj_mm(3, 0)
+        sort_counts(7, G, True)
+        unit(5)
+        transpose_counts(6)
+        proj_pair(2, 2, S)
+        proj_mm(3, 2)
+        inverse_rate(6)
+        proj_pair(3, 0, S)
+        q_proj(2)
+        q_res(5)
+        proj_pair(3, 2, S)
+        inverse_rate(7)
+        multiply(6, 0)
+        multiply(6, 1)
+        for g in range(2):
+            for m in range(3):
+                out_matmul(m, g)
+        transpose_counts(7)
+        out_matmul(3, 0)
+        out_matmul(3, 1)
+        for m in range(SLOTS):
+            out_matmul(m, 2)
+        subtract(6, 0)
+        q_proj(3)
+        for m in range(SLOTS):
+            out_matmul(m, GROUPS - 1)
+        subtract(6, 1)
+        last = UNITS - 1
+        multiply(last, 0)
+        q_res(6)
+        multiply(last, 1)
+        for g in range(GROUPS - 1):
+            out_matmul(SLOTS, g)
+        for m in range(SLOTS):
+            out_store(m, S)
+            if m < SLOTS - 1:
+                for g in range(GROUPS - 1):
+                    out_matmul(SLOTS + 1 + m, g)
+        subtract(last, 0)
+        subtract(last, 1)
+        for piece in range(2):
+            quantize(("res", last), res_grouped[last], piece * PIECE, (piece + 1) * PIECE)
+            out_matmul(SLOTS + 2 * piece, GROUPS - 1)
+            out_matmul(SLOTS + 2 * piece + 1, GROUPS - 1)
+        out_store(4, S)
+        out_store(5, V)
+        out_store(6, S)
+        out_store(7, V)

@@ -68,8 +68,8 @@ def tile_spatial_poisson_program_gradient_s12_kernel(
         warm = kept("warm", [P, 1], F32)
         warm_out = kept("warm_out", [P, 1], F32)
 
-        nc.vector.memset(a_scales[:].bitcast(I32), 0)
         nc.vector.memset(s_scales_raw[:].bitcast(I32), 0)
+        nc.vector.memset(a_scales[:].bitcast(I32), 0)
         nc.vector.memset(warm[:], 1.0)
         nc.vector.memset(bg_sorted[:], 0.0)
         nc.vector.memset(weight_sorted[:], 0.0)
@@ -119,14 +119,14 @@ def tile_spatial_poisson_program_gradient_s12_kernel(
                 )
 
         make_identity(nc, ident[:])
-        load_scales(nc.gpsimd, a_scales, abn_scales)
+        nc.gpsimd.dma_start(out=bg_raw[:], in_=bg.rearrange("(g n) -> g n", g=GROUPS))
         nc.gpsimd.dma_start(out=weight_raw[:], in_=gene_w.rearrange("(g n) -> g n", g=GROUPS))
 
+        load_prog(0)
         load_s(0)
         load_a(0)
-        nc.sync.dma_start(out=bg_raw[:], in_=bg.rearrange("(g n) -> g n", g=GROUPS))
-        load_prog(0)
         load_scales(nc.sync, s_scales_raw, sigq_scales)
+        load_scales(nc.sync, a_scales, abn_scales)
         load_s(1)
         load_prog(1)
         load_counts(0)
@@ -283,16 +283,16 @@ def tile_spatial_poisson_program_gradient_s12_kernel(
             )
             quot[(u, piece)] = dst
 
-        def subtract(u, piece):
+        def subtract(u, piece, lo=0, hi=PIECE):
             g = u % GROUPS
-            if piece == 0:
+            if u not in res_grouped:
                 res_grouped[u] = rotating("res_grouped", u, [P, PASS * SLOTS], BF16, 2)
-            part = res_grouped[u][:, piece * PIECE * SLOTS:(piece + 1) * PIECE * SLOTS]
+            part = res_grouped[u][:, (piece * PIECE + lo) * SLOTS:(piece * PIECE + hi) * SLOTS]
             weights = weight_t[:, :, g:g + 1].rearrange("p t (x i) -> p x t i", x=1)
             nc.vector.tensor_tensor(
                 out=part.rearrange("p (x i t) -> p x t i", i=2, t=SLOTS),
-                in0=quot[(u, piece)][:].rearrange("p t (x i) -> p x t i", i=2),
-                in1=weights.to_broadcast([P, PIECE // 2, SLOTS, 2]),
+                in0=quot[(u, piece)][:, :, lo:hi].rearrange("p t (x i) -> p x t i", i=2),
+                in1=weights.to_broadcast([P, (hi - lo) // 2, SLOTS, 2]),
                 op=ALU.subtract,
             )
 
@@ -378,8 +378,8 @@ def tile_spatial_poisson_program_gradient_s12_kernel(
 
         bg_t = vector_columns(bg_raw, bg_sorted, "acc0")
         nc.scalar.copy(out=bg_col[:], in_=bg_t[:, :, :GROUPS])
-        sort_s(0)
         interleave_prog(0, V)
+        sort_s(0)
         sort_s_scales()
         for n in range(MU_BANKS):
             mu_matmul(n)
@@ -505,12 +505,16 @@ def tile_spatial_poisson_program_gradient_s12_kernel(
                 for g in range(GROUPS - 1):
                     out_matmul(SLOTS + 1 + m, g)
         subtract(last, 0)
-        subtract(last, 1)
-        for piece in range(2):
-            quantize(("res", last), res_grouped[last], piece * PIECE, (piece + 1) * PIECE)
-            out_matmul(SLOTS + 2 * piece, GROUPS - 1)
-            out_matmul(SLOTS + 2 * piece + 1, GROUPS - 1)
+        subtract(last, 1, 0, P)
+        quantize(("res", last), res_grouped[last], 0, PIECE)
+        out_matmul(4, GROUPS - 1)
+        out_matmul(5, GROUPS - 1)
+        subtract(last, 1, P, PIECE)
         out_store(4, S)
-        out_store(5, V)
-        out_store(6, S)
-        out_store(7, V)
+        out_store(5, S)
+        quantize(("res", last), res_grouped[last], PIECE, PIECE + P)
+        out_matmul(6, GROUPS - 1)
+        quantize(("res", last), res_grouped[last], PIECE + P, PASS)
+        out_matmul(7, GROUPS - 1)
+        out_store(6, V)
+        out_store(7, S)

@@ -13,19 +13,27 @@ U32 = mybir.dt.uint32
 U8 = mybir.dt.uint8
 FP8X4 = mybir.dt.float8_e4m3fn_x4
 FP4X4 = mybir.dt.float4_e2m1fn_x4
-ACT = mybir.ActivationFunctionType
+FUNC = mybir.ActivationFunctionType
 ALU = mybir.AluOpType
 
 P = 128
 SLOTS = 4
 PASS = P * SLOTS
+RUN = 8
+QUADRANTS = 4
 K_PASSES = K // PASS
 GROUPS = N // PASS
-HALVES = M // PASS
-UNITS = HALVES * GROUPS
+UNITS = (M // PASS) * GROUPS
+TILES = PASS // P
 PIECE = PASS // 2
 MU_BANKS = 3
-RECIP_BUFS = 4
+
+ROW_BUFS = 8
+COUNT_BUFS = 6
+INVERSE_BUFS = 4
+RESULT_BUFS = 4
+
+VECTOR, SCALAR, GPSIMD = "vector", "scalar", "gpsimd"
 
 
 def tile_spatial_poisson_program_gradient_s12_kernel(
@@ -42,16 +50,19 @@ def tile_spatial_poisson_program_gradient_s12_kernel(
         def kept(name, shape, dtype):
             return keep.tile(shape, dtype, name=name, tag=name, align_bytes=64)
 
-        def rotating(tag, index, shape, dtype, bufs):
-            return work.tile(shape, dtype, name="%s_%d" % (tag, index), tag=tag, bufs=bufs, align_bytes=64)
+        def rotating(tag, name, shape, dtype, bufs=2):
+            return work.tile(shape, dtype, name=name, tag=tag, bufs=bufs, align_bytes=64)
+
+        def released(name, shape):
+            return rotating("released", name, shape, BF16, 1)
 
         def bank(tag, name, shape, dtype):
             return psum.tile(shape, dtype, name=name, tag=tag)
 
         def copy_on(engine, dst, src):
-            if engine == "vector":
+            if engine == VECTOR:
                 nc.vector.tensor_copy(out=dst, in_=src)
-            elif engine == "gpsimd":
+            elif engine == GPSIMD:
                 nc.gpsimd.tensor_scalar(out=dst, in0=src, scalar1=1.0, scalar2=0.0, op0=ALU.mult, op1=ALU.add)
             else:
                 nc.scalar.copy(out=dst, in_=src)
@@ -73,7 +84,7 @@ def tile_spatial_poisson_program_gradient_s12_kernel(
         nc.vector.memset(warm[:], 1.0)
         nc.vector.memset(bg_sorted[:], 0.0)
         nc.vector.memset(weight_sorted[:], 0.0)
-        nc.scalar.activation(out=warm_out[:], in_=warm[:], func=ACT.Ln)
+        nc.scalar.activation(out=warm_out[:], in_=warm[:], func=FUNC.Ln)
 
         rows_raw = {}
         counts_raw = {}
@@ -81,7 +92,7 @@ def tile_spatial_poisson_program_gradient_s12_kernel(
         a_words = {}
 
         def load_rows(key, rows):
-            raw = rotating("rows_raw", len(rows_raw), [P, SLOTS, PASS], BF16, 8)
+            raw = rotating("rows_raw", "rows_raw_%s_%d" % key, [P, SLOTS, PASS], BF16, ROW_BUFS)
             nc.sync.dma_start(out=raw[:], in_=rows.rearrange("(p j) w -> p j w", j=SLOTS))
             rows_raw[key] = raw
 
@@ -92,9 +103,9 @@ def tile_spatial_poisson_program_gradient_s12_kernel(
             load_rows((g, c), sig[c * PASS:(c + 1) * PASS, g * PASS:(g + 1) * PASS])
 
         def load_counts(u):
-            h, g = divmod(u, GROUPS)
-            raw = rotating("counts_raw", u, [P, SLOTS, PASS], BF16, 6)
-            rows = counts_w[h * PASS:(h + 1) * PASS, g * PASS:(g + 1) * PASS]
+            half, g = divmod(u, GROUPS)
+            raw = rotating("counts_raw", "counts_raw_%d" % u, [P, TILES, PASS], BF16, COUNT_BUFS)
+            rows = counts_w[half * PASS:(half + 1) * PASS, g * PASS:(g + 1) * PASS]
             nc.sync.dma_start(out=raw[:], in_=rows.rearrange("(s p) n -> p s n", p=P))
             counts_raw[u] = raw
 
@@ -107,30 +118,31 @@ def tile_spatial_poisson_program_gradient_s12_kernel(
         def load_s(g):
             s_raw[g] = load_words(sigq_words, g, "s_raw")
 
-        def load_a(h):
-            a_words[h] = load_words(abn_words, h, "a_words")
+        def load_a(half):
+            a_words[half] = load_words(abn_words, half, "a_words")
 
-        def load_scales(queue, plane, scales):
+        def load_scales(plane, scales, quadrants):
             view = plane[:].rearrange("p (c n) -> p c n", c=K_PASSES)
-            for quad in range(4):
-                queue.dma_start(
+            for quad in quadrants:
+                nc.sync.dma_start(
                     out=view[32 * quad:32 * quad + 4, :, :].bitcast(I32),
                     in_=scales[:, 4 * quad:4 * quad + 4, :].rearrange("c r n -> r c n").bitcast(I32),
                 )
 
-        make_identity(nc, ident[:])
         nc.gpsimd.dma_start(out=bg_raw[:], in_=bg.rearrange("(g n) -> g n", g=GROUPS))
         nc.gpsimd.dma_start(out=weight_raw[:], in_=gene_w.rearrange("(g n) -> g n", g=GROUPS))
+        make_identity(nc, ident[:])
 
-        load_prog(0)
         load_s(0)
         load_a(0)
-        load_scales(nc.sync, s_scales_raw, sigq_scales)
-        load_scales(nc.sync, a_scales, abn_scales)
+        load_scales(s_scales_raw, sigq_scales, range(QUADRANTS))
+        load_scales(a_scales, abn_scales, range(1))
+        load_prog(0)
+        load_scales(a_scales, abn_scales, range(1, QUADRANTS))
         load_s(1)
         load_prog(1)
-        load_counts(0)
         load_sig(0, 0)
+        load_counts(0)
         load_s(2)
         load_sig(0, 1)
         load_counts(1)
@@ -151,12 +163,22 @@ def tile_spatial_poisson_program_gradient_s12_kernel(
         counts_sorted = {}
         counts_t = {}
         mu = {}
-        recip = {}
-        quot = {}
+        inverse = {}
+        ratio = {}
         res_grouped = {}
         proj_grouped = {}
         proj_bank = {}
         out_bank = {}
+
+        def vector_columns(raw, sorted_rows, tag):
+            nc.scalar.copy(
+                out=sorted_rows[:GROUPS, :].rearrange("p (t q r) -> p t q r", t=SLOTS, r=RUN),
+                in_=raw[:].rearrange("p (q t r) -> p t q r", t=SLOTS, r=RUN),
+            )
+            dst = bank(tag, "columns_" + tag, [P, SLOTS, P], BF16)
+            for t in range(SLOTS):
+                nc.tensor.transpose(dst[:, t, :], sorted_rows[:, t * P:(t + 1) * P], ident[:])
+            return dst
 
         def sort_s(g):
             dst = kept("s_words_%d" % g, [P, SLOTS, K_PASSES * 2 * P], U8)
@@ -173,43 +195,38 @@ def tile_spatial_poisson_program_gradient_s12_kernel(
                 in_=s_scales_raw[:].bitcast(I32).rearrange("p (x t w) -> p t x w", t=SLOTS, w=2),
             )
 
-        def interleave_prog(c, engine):
+        def interleave_prog(c):
             key = ("prog", c)
-            dst = rotating("grouped", len(grouped), [P, PASS * SLOTS], BF16, 2)
-            copy_on(
-                engine,
-                dst[:].rearrange("p (x i j) -> p x j i", i=4, j=SLOTS),
-                rows_raw[key][:].rearrange("p j (x i) -> p x j i", i=4),
+            dst = rotating("grouped", "grouped_prog_%d" % c, [P, PASS * SLOTS], BF16)
+            nc.vector.tensor_copy(
+                out=dst[:].rearrange("p (x i j) -> p x j i", i=4, j=SLOTS),
+                in_=rows_raw[key][:].rearrange("p j (x i) -> p x j i", i=4),
             )
             grouped[key] = dst
 
-        def interleave_sig(g, c, engine, gate=False):
-            key = (g, c)
-            if gate:
-                dst = rotating("grouped_gpsimd", len(grouped), [P, PASS * SLOTS], BF16, 1)
-            else:
-                dst = rotating("grouped", len(grouped), [P, PASS * SLOTS], BF16, 2)
-            dst_view = dst[:].rearrange("p (t q a i j) -> p a q t j i", t=SLOTS, a=2, i=4, j=SLOTS)
-            src_view = rows_raw[key][:].rearrange("p j (q t a i) -> p a q t j i", t=SLOTS, a=2, i=4)
-            if engine == "gpsimd":
-                nc.gpsimd.tensor_scalar(
-                    out=dst[:].rearrange("p (t q r j) -> p q t r j", t=SLOTS, r=8, j=SLOTS),
-                    in0=rows_raw[key][:].rearrange("p j (q t r) -> p q t r j", t=SLOTS, r=8),
-                    scalar1=1.0, scalar2=0.0, op0=ALU.mult, op1=ALU.add,
+        def interleave_sig(g, c, engine, timed):
+            name = "grouped_%d_%d" % (g, c)
+            shape = [P, PASS * SLOTS]
+            dst = released(name, shape) if timed else rotating("grouped", name, shape, BF16)
+            raw = rows_raw[(g, c)]
+            if engine == GPSIMD:
+                copy_on(
+                    engine,
+                    dst[:].rearrange("p (t q r j) -> p q t r j", t=SLOTS, r=RUN, j=SLOTS),
+                    raw[:].rearrange("p j (q t r) -> p q t r j", t=SLOTS, r=RUN),
                 )
             else:
+                dst_view = dst[:].rearrange("p (t q a i j) -> p a q t j i", t=SLOTS, a=2, i=4, j=SLOTS)
+                src_view = raw[:].rearrange("p j (q t a i) -> p a q t j i", t=SLOTS, a=2, i=4)
                 for a in range(2):
                     copy_on(engine, dst_view[:, a], src_view[:, a])
-            grouped[key] = dst
-
-        def code_tiles(key):
-            if key not in codes:
-                name = "_".join(str(part) for part in key)
-                codes[key] = (kept("codes_" + name, [P, PASS], U32), kept("scales_" + name, [P, PASS], U8))
-            return codes[key]
+            grouped[(g, c)] = dst
 
         def quantize(key, src, start=0, stop=PASS):
-            words, scales = code_tiles(key)
+            if key not in codes:
+                name = "%s_%d" % key
+                codes[key] = (kept("codes_" + name, [P, PASS], U32), kept("scales_" + name, [P, PASS], U8))
+            words, scales = codes[key]
             nc.vector.quantize_mx(
                 out=words[:, start:stop].bitcast(FP8X4),
                 scales=scales[:, start:stop],
@@ -219,16 +236,21 @@ def tile_spatial_poisson_program_gradient_s12_kernel(
         def quantize_rows(key):
             quantize(key, grouped[key])
 
-        def sort_counts(u, engine, gate=False):
-            if gate:
-                dst = rotating("grouped_gpsimd", 100 + u, [P, SLOTS, PASS], BF16, 1)
-            else:
-                dst = rotating("counts_sorted", u, [P, SLOTS, PASS], BF16, 2)
+        def quantize_res(u, start=0, stop=PASS):
+            quantize(("res", u), res_grouped[u], start, stop)
+
+        def quantize_proj(g):
+            quantize(("proj", g), proj_grouped[g])
+
+        def sort_counts(u, engine):
+            name = "counts_sorted_%d" % u
+            shape = [P, SLOTS, PASS]
+            dst = released(name, shape) if engine == GPSIMD else rotating("counts_sorted", name, shape, BF16)
             src = counts_raw[u][:].rearrange("p s n -> p (s n)")
             copy_on(
                 engine,
-                dst[:].rearrange("p t (x r) -> p t x r", r=8),
-                src.rearrange("p (x t r) -> p t x r", t=SLOTS, r=8),
+                dst[:].rearrange("p t (x r) -> p t x r", r=RUN),
+                src.rearrange("p (x t r) -> p t x r", t=SLOTS, r=RUN),
             )
             counts_sorted[u] = dst
 
@@ -236,99 +258,110 @@ def tile_spatial_poisson_program_gradient_s12_kernel(
             for piece in range(2):
                 dst = bank("counts_t%d" % piece, "counts_t_%d_%d" % (u, piece), [P, SLOTS, PIECE], BF16)
                 for t in range(SLOTS):
-                    for s in range(2):
+                    for s in range(PIECE // P):
                         col = piece * PIECE + s * P
                         nc.tensor.transpose(dst[:, t, s * P:(s + 1) * P], counts_sorted[u][:, t, col:col + P], ident[:])
                 counts_t[(u, piece)] = dst
 
         def mu_matmul(n):
-            if n >= UNITS * SLOTS:
-                return
             u, t = divmod(n, SLOTS)
-            h, g = divmod(u, GROUPS)
+            half, g = divmod(u, GROUPS)
             dst = bank("mu%d" % (n % MU_BANKS), "mu_%d" % n, [P, PASS], F32)
             for c in range(K_PASSES):
                 s_col = (c * GROUPS + g) * P
-                a_col = c * M + h * PASS
+                a_col = c * M + half * PASS
                 nc.tensor.matmul_mx(
                     out=dst[:],
                     lhsT=s_words[g][:, t, c * 2 * P:(c + 1) * 2 * P].bitcast(FP4X4),
                     lhsT_scale=s_scales[:, t, s_col:s_col + P],
-                    rhs=a_words[h][:, c, :].bitcast(FP4X4),
+                    rhs=a_words[half][:, c, :].bitcast(FP4X4),
                     rhs_scale=a_scales[:, a_col:a_col + PASS],
                     start=(c == 0),
                     stop=(c == K_PASSES - 1),
                 )
             mu[n] = dst
 
-        def log_rate(u, ahead=SLOTS):
+        def log_rate(u, refills=SLOTS):
             g = u % GROUPS
-            dst = rotating("recip", u, [P, SLOTS, PASS], F32, RECIP_BUFS)
-            recip[u] = dst
+            dst = rotating("inverse", "inverse_%d" % u, [P, SLOTS, PASS], F32, INVERSE_BUFS)
+            inverse[u] = dst
             for t in range(SLOTS):
                 n = u * SLOTS + t
-                nc.scalar.activation(out=dst[:, t, :], in_=mu[n][:], func=ACT.Ln, bias=bg_col[:, t, g:g + 1])
-                if t < ahead:
+                nc.scalar.activation(out=dst[:, t, :], in_=mu[n][:], func=FUNC.Ln, bias=bg_col[:, t, g:g + 1])
+                if t < refills:
                     mu_matmul(n + MU_BANKS)
 
         def inverse_rate(u):
             for piece in range(2):
-                part = recip[u][:, :, piece * PIECE:(piece + 1) * PIECE]
-                nc.scalar.activation(out=part, in_=part, func=ACT.Exp, scale=-1.0)
+                part = inverse[u][:, :, piece * PIECE:(piece + 1) * PIECE]
+                nc.scalar.activation(out=part, in_=part, func=FUNC.Exp, scale=-1.0)
 
         def multiply(u, piece):
-            dst = rotating("quot", 2 * u + piece, [P, SLOTS, PIECE], F32, 2)
+            dst = rotating("ratio", "ratio_%d_%d" % (u, piece), [P, SLOTS, PIECE], F32)
             nc.vector.tensor_tensor(
-                out=dst[:], in0=counts_t[(u, piece)][:], in1=recip[u][:, :, piece * PIECE:(piece + 1) * PIECE], op=ALU.mult
+                out=dst[:],
+                in0=inverse[u][:, :, piece * PIECE:(piece + 1) * PIECE],
+                in1=counts_t[(u, piece)][:],
+                op=ALU.mult,
             )
-            quot[(u, piece)] = dst
+            ratio[(u, piece)] = dst
 
         def subtract(u, piece, lo=0, hi=PIECE):
             g = u % GROUPS
             if u not in res_grouped:
-                res_grouped[u] = rotating("res_grouped", u, [P, PASS * SLOTS], BF16, 2)
+                res_grouped[u] = rotating("res_grouped", "res_grouped_%d" % u, [P, PASS * SLOTS], BF16)
             part = res_grouped[u][:, (piece * PIECE + lo) * SLOTS:(piece * PIECE + hi) * SLOTS]
             weights = weight_t[:, :, g:g + 1].rearrange("p t (x i) -> p x t i", x=1)
             nc.vector.tensor_tensor(
                 out=part.rearrange("p (x i t) -> p x t i", i=2, t=SLOTS),
-                in0=quot[(u, piece)][:, :, lo:hi].rearrange("p t (x i) -> p x t i", i=2),
+                in0=ratio[(u, piece)][:, :, lo:hi].rearrange("p t (x i) -> p x t i", i=2),
                 in1=weights.to_broadcast([P, (hi - lo) // 2, SLOTS, 2]),
                 op=ALU.subtract,
             )
 
-        proj_tags = {(2, 2): "mu2", (2, 3): "mu0", (3, 2): "mu1", (3, 3): "mu2"}
+        def residual(u):
+            multiply(u, 0)
+            multiply(u, 1)
+            subtract(u, 0)
+            subtract(u, 1)
 
-        def proj_matmul(g, b):
-            dst = bank(proj_tags.get((g, b), "acc%d" % (b % 2)), "proj_%d_%d" % (g, b), [P, SLOTS, P], F32)
-            cols = slice(b * P, (b + 1) * P)
-            for t in range(SLOTS):
-                genes = slice(t * P, (t + 1) * P)
-                for c in range(K_PASSES):
-                    nc.tensor.matmul_mx(
-                        out=dst[:, t, :],
-                        lhsT=codes[(g, c)][0][:, genes].bitcast(FP8X4),
-                        lhsT_scale=codes[(g, c)][1][:, genes],
-                        rhs=codes[("prog", c)][0][:, cols].bitcast(FP8X4),
-                        rhs_scale=codes[("prog", c)][1][:, cols],
-                        start=(c == 0),
-                        stop=(c == K_PASSES - 1),
-                    )
-            proj_bank[(g, b)] = dst
+        def proj_matmuls(g, first, tags=("acc0", "acc1")):
+            for b, tag in zip((first, first + 1), tags):
+                dst = bank(tag, "proj_%d_%d" % (g, b), [P, SLOTS, P], F32)
+                programs = slice(b * P, (b + 1) * P)
+                for t in range(SLOTS):
+                    genes = slice(t * P, (t + 1) * P)
+                    for c in range(K_PASSES):
+                        nc.tensor.matmul_mx(
+                            out=dst[:, t, :],
+                            lhsT=codes[(g, c)][0][:, genes].bitcast(FP8X4),
+                            lhsT_scale=codes[(g, c)][1][:, genes],
+                            rhs=codes[("prog", c)][0][:, programs].bitcast(FP8X4),
+                            rhs_scale=codes[("prog", c)][1][:, programs],
+                            start=(c == 0),
+                            stop=(c == K_PASSES - 1),
+                        )
+                proj_bank[(g, b)] = dst
 
-        def proj_copy(g, b, engine):
-            if b == 0:
-                proj_grouped[g] = rotating("proj_grouped", g, [P, R * SLOTS], BF16, 2)
-            part = proj_grouped[g][:, b * P * SLOTS:(b + 1) * P * SLOTS]
-            copy_on(engine, part.rearrange("p (r t) -> p r t", t=SLOTS), proj_bank[(g, b)][:].rearrange("p t r -> p r t"))
+        def proj_copies(g, first, engine):
+            if first == 0:
+                proj_grouped[g] = rotating("proj_grouped", "proj_grouped_%d" % g, [P, R * SLOTS], BF16)
+            for b in (first, first + 1):
+                part = proj_grouped[g][:, b * P * SLOTS:(b + 1) * P * SLOTS]
+                copy_on(
+                    engine,
+                    part.rearrange("p (r t) -> p r t", t=SLOTS),
+                    proj_bank[(g, b)][:].rearrange("p t r -> p r t"),
+                )
 
-        out_tags = ["mu0", "acc0", "acc1", "mu1", "mu2", "mu0", "acc0", "acc1"]
+        out_tags = ["mu0", "acc0", "acc1", "mu1", "mu2"]
 
         def out_matmul(m, g):
-            h, s = divmod(m, SLOTS)
+            half, s = divmod(m, TILES)
             if g == 0:
-                out_bank[m] = bank(out_tags[m], "out_%d" % m, [P, R], F32)
+                out_bank[m] = bank(out_tags[m % len(out_tags)], "out_%d" % m, [P, R], F32)
             spots = slice(s * P, (s + 1) * P)
-            words, scales = codes[("res", h * GROUPS + g)]
+            words, scales = codes[("res", half * GROUPS + g)]
             nc.tensor.matmul_mx(
                 out=out_bank[m][:],
                 lhsT=words[:, spots].bitcast(FP8X4),
@@ -340,181 +373,151 @@ def tile_spatial_poisson_program_gradient_s12_kernel(
             )
 
         def out_store(m, engine):
-            result = rotating("result", m, [P, R], F32, 4)
+            result = rotating("result", "result_%d" % m, [P, R], F32, RESULT_BUFS)
             copy_on(engine, result[:], out_bank[m][:])
             nc.sync.dma_start(out=out[m * P:(m + 1) * P, :], in_=result[:])
 
-        V, S, G = "vector", "scalar", "gpsimd"
-
-        def unit(u):
-            multiply(u, 0)
-            multiply(u, 1)
-            subtract(u, 0)
-            subtract(u, 1)
-
-        def proj_pair(g, b, engine):
-            proj_copy(g, b, engine)
-            proj_copy(g, b + 1, engine)
-
-        def proj_mm(g, b):
-            proj_matmul(g, b)
-            proj_matmul(g, b + 1)
-
-        def q_res(u):
-            quantize(("res", u), res_grouped[u])
-
-        def q_proj(g):
-            quantize(("proj", g), proj_grouped[g])
-
-        def vector_columns(raw, sorted_rows, tag):
-            nc.scalar.copy(
-                out=sorted_rows[:GROUPS, :].rearrange("p (t q r) -> p t q r", t=SLOTS, r=8),
-                in_=raw[:].rearrange("p (q t r) -> p t q r", t=SLOTS, r=8),
-            )
-            dst = bank(tag, "columns_" + tag, [P, SLOTS, P], BF16)
-            for t in range(SLOTS):
-                nc.tensor.transpose(dst[:, t, :], sorted_rows[:, t * P:(t + 1) * P], ident[:])
-            return dst
 
         bg_t = vector_columns(bg_raw, bg_sorted, "acc0")
         nc.scalar.copy(out=bg_col[:], in_=bg_t[:, :, :GROUPS])
-        interleave_prog(0, V)
+        weight_t = vector_columns(weight_raw, weight_sorted, "weights")
         sort_s(0)
         sort_s_scales()
         for n in range(MU_BANKS):
             mu_matmul(n)
-        quantize_rows(("prog", 0))
+        interleave_prog(0)
         sort_s(1)
         log_rate(0)
-        interleave_prog(1, V)
+        quantize_rows(("prog", 0))
+        interleave_prog(1)
         load_sig(3, 0)
         load_sig(3, 1)
-        sort_counts(0, V)
-        load_counts(6)
+        interleave_sig(0, 0, VECTOR, timed=False)
         quantize_rows(("prog", 1))
-        interleave_sig(0, 0, V)
-        log_rate(1, 1)
-        weight_t = vector_columns(weight_raw, weight_sorted, "weights")
+        sort_counts(0, VECTOR)
+        load_counts(6)
+        log_rate(1, refills=1)
         transpose_counts(0)
         sort_s(2)
-        mu_matmul(8)
-        mu_matmul(9)
-        mu_matmul(10)
+        for n in range(2 * SLOTS, 2 * SLOTS + MU_BANKS):
+            mu_matmul(n)
         quantize_rows((0, 0))
-        interleave_sig(0, 1, V, True)
-        sort_counts(1, V)
+        interleave_sig(0, 1, VECTOR, timed=True)
+        sort_counts(1, VECTOR)
         load_counts(7)
         sort_s(3)
         quantize_rows((0, 1))
         inverse_rate(0)
         inverse_rate(1)
-        proj_mm(0, 0)
-        interleave_sig(1, 0, G, True)
-        interleave_sig(1, 1, G)
+        proj_matmuls(0, 0)
+
+        interleave_sig(1, 0, GPSIMD, timed=True)
+        interleave_sig(1, 1, GPSIMD, timed=False)
         multiply(0, 0)
         multiply(0, 1)
         transpose_counts(1)
-        proj_pair(0, 0, V)
-        proj_mm(0, 2)
+        proj_copies(0, 0, VECTOR)
+        proj_matmuls(0, 2)
         subtract(0, 0)
         subtract(0, 1)
-        proj_pair(0, 2, V)
+        proj_copies(0, 2, VECTOR)
         log_rate(2)
-        sort_counts(2, V)
-        q_res(0)
+        sort_counts(2, VECTOR)
+        quantize_res(0)
         quantize_rows((1, 1))
         quantize_rows((1, 0))
-        interleave_sig(2, 0, G, True)
+
+        interleave_sig(2, 0, GPSIMD, timed=True)
         log_rate(3)
-        unit(1)
+        residual(1)
         log_rate(4)
         transpose_counts(2)
-        proj_mm(1, 0)
-        q_proj(0)
-        q_res(1)
-        sort_counts(3, V)
+        proj_matmuls(1, 0)
+        quantize_proj(0)
+        quantize_res(1)
+        sort_counts(3, VECTOR)
         quantize_rows((2, 0))
         inverse_rate(2)
-        interleave_sig(2, 1, G, True)
-        unit(2)
+
+        interleave_sig(2, 1, GPSIMD, timed=True)
+        residual(2)
         transpose_counts(3)
-        proj_pair(1, 0, S)
-        proj_mm(1, 2)
+        proj_copies(1, 0, SCALAR)
+        proj_matmuls(1, 2)
         inverse_rate(3)
-        proj_pair(1, 2, S)
         inverse_rate(4)
-        sort_counts(4, V)
-        q_res(2)
+        proj_copies(1, 2, SCALAR)
+        sort_counts(4, VECTOR)
+        quantize_res(2)
         quantize_rows((2, 1))
-        proj_mm(2, 0)
-        interleave_sig(3, 0, G, True)
-        unit(3)
-        transpose_counts(4)
+        proj_matmuls(2, 0)
+
+        interleave_sig(3, 0, GPSIMD, timed=True)
+        residual(3)
         log_rate(5)
+        transpose_counts(4)
+        proj_copies(2, 0, SCALAR)
         log_rate(6)
-        sort_counts(5, V)
-        q_proj(1)
-        q_res(3)
+        sort_counts(5, VECTOR)
+        quantize_proj(1)
+        quantize_res(3)
         quantize_rows((3, 0))
-        interleave_sig(3, 1, G, True)
-        unit(4)
-        log_rate(7)
+
+        interleave_sig(3, 1, GPSIMD, timed=True)
+        residual(4)
+        log_rate(7, refills=1)
         transpose_counts(5)
-        proj_mm(2, 2)
+        proj_matmuls(2, 2, ("mu2", "mu0"))
         inverse_rate(5)
-        proj_pair(2, 0, S)
-        sort_counts(6, V)
-        q_res(4)
+        sort_counts(6, VECTOR)
+        quantize_res(4)
         quantize_rows((3, 1))
-        proj_mm(3, 0)
-        sort_counts(7, G, True)
-        unit(5)
+        proj_matmuls(3, 0)
+
+        sort_counts(7, GPSIMD)
+        residual(5)
         transpose_counts(6)
-        proj_pair(2, 2, S)
-        proj_mm(3, 2)
+        proj_copies(2, 2, SCALAR)
+        proj_matmuls(3, 2, ("mu1", "mu2"))
         inverse_rate(6)
-        proj_pair(3, 0, S)
-        q_proj(2)
-        q_res(5)
-        proj_pair(3, 2, S)
+        proj_copies(3, 0, SCALAR)
+        quantize_proj(2)
+        quantize_res(5)
+        proj_copies(3, 2, SCALAR)
         inverse_rate(7)
+
         multiply(6, 0)
         multiply(6, 1)
-        for g in range(2):
-            for m in range(3):
+        quantize_proj(3)
+        for g in range(GROUPS):
+            for m in range(TILES):
                 out_matmul(m, g)
-        transpose_counts(7)
-        out_matmul(3, 0)
-        out_matmul(3, 1)
-        for m in range(SLOTS):
-            out_matmul(m, 2)
+            if g == GROUPS // 2 - 1:
+                transpose_counts(7)
         subtract(6, 0)
-        q_proj(3)
-        for m in range(SLOTS):
-            out_matmul(m, GROUPS - 1)
         subtract(6, 1)
+
         last = UNITS - 1
         multiply(last, 0)
-        q_res(6)
-        multiply(last, 1)
-        for g in range(GROUPS - 1):
-            out_matmul(SLOTS, g)
-        for m in range(SLOTS):
-            out_store(m, S)
-            if m < SLOTS - 1:
-                for g in range(GROUPS - 1):
-                    out_matmul(SLOTS + 1 + m, g)
+        quantize_res(last - 1)
+        for m in range(TILES):
+            out_matmul(TILES + m, 0)
+            out_matmul(TILES + m, 1)
+            out_store(m, SCALAR)
+        for m in range(TILES):
+            out_matmul(TILES + m, 2)
         subtract(last, 0)
+        multiply(last, 1)
+        quantize_res(last, 0, PIECE)
+        out_matmul(TILES, GROUPS - 1)
+        out_matmul(TILES + 1, GROUPS - 1)
         subtract(last, 1, 0, P)
-        quantize(("res", last), res_grouped[last], 0, PIECE)
-        out_matmul(4, GROUPS - 1)
-        out_matmul(5, GROUPS - 1)
         subtract(last, 1, P, PIECE)
-        out_store(4, S)
-        out_store(5, S)
-        quantize(("res", last), res_grouped[last], PIECE, PIECE + P)
-        out_matmul(6, GROUPS - 1)
-        quantize(("res", last), res_grouped[last], PIECE + P, PASS)
-        out_matmul(7, GROUPS - 1)
-        out_store(6, V)
-        out_store(7, S)
+        out_store(TILES, SCALAR)
+        out_store(TILES + 1, SCALAR)
+        quantize_res(last, PIECE, PIECE + P)
+        out_matmul(TILES + 2, GROUPS - 1)
+        quantize_res(last, PIECE + P, PASS)
+        out_matmul(TILES + 3, GROUPS - 1)
+        out_store(TILES + 2, SCALAR)
+        out_store(TILES + 3, VECTOR)

from contextlib import ExitStack

import concourse.mybir as mybir
from concourse.masks import make_identity

M, K, N, R = 1024, 1024, 2048, 512
FLOPS = 2 * (M * N * K + N * R * K + M * R * N)

F32 = mybir.dt.float32
BF16 = mybir.dt.bfloat16
I32 = mybir.dt.int32
U32 = mybir.dt.uint32
U8 = mybir.dt.uint8
FP8X4 = mybir.dt.float8_e4m3fn_x4
FP4X4 = mybir.dt.float4_e2m1fn_x4
FUNC = mybir.ActivationFunctionType
ALU = mybir.AluOpType

P = 128
SLOTS = 4
PASS = P * SLOTS
RUN = 8
QUADRANTS = 4
K_PASSES = K // PASS
GROUPS = N // PASS
UNITS = (M // PASS) * GROUPS
TILES = PASS // P
PIECE = PASS // 2
MU_BANKS = 3

ROW_BUFS = 8
COUNT_BUFS = 6
INVERSE_BUFS = 4
RESULT_BUFS = 4

VECTOR, SCALAR, GPSIMD = "vector", "scalar", "gpsimd"


def tile_spatial_poisson_program_gradient_s12_kernel(
    tc, abn_words, abn_scales, sigq_words, sigq_scales, bg, counts_w, gene_w, sig, prog, out
):
    nc = tc.nc

    with ExitStack() as ctx:
        keep = ctx.enter_context(tc.tile_pool(name="keep", bufs=1))
        work = ctx.enter_context(tc.tile_pool(name="work", bufs=2))
        psum = ctx.enter_context(tc.psum_pool(name="psum", bufs=1))
        ctx.enter_context(tc.manual_schedule())

        def kept(name, shape, dtype):
            return keep.tile(shape, dtype, name=name, tag=name, align_bytes=64)

        def rotating(tag, name, shape, dtype, bufs=2):
            return work.tile(shape, dtype, name=name, tag=tag, bufs=bufs, align_bytes=64)

        def released(name, shape):
            return rotating("released", name, shape, BF16, 1)

        def bank(tag, name, shape, dtype):
            return psum.tile(shape, dtype, name=name, tag=tag)

        def copy_on(engine, dst, src):
            if engine == VECTOR:
                nc.vector.tensor_copy(out=dst, in_=src)
            elif engine == GPSIMD:
                nc.gpsimd.tensor_scalar(out=dst, in0=src, scalar1=1.0, scalar2=0.0, op0=ALU.mult, op1=ALU.add)
            else:
                nc.scalar.copy(out=dst, in_=src)

        a_scales = kept("a_scales", [P, K_PASSES * M], U8)
        s_scales_raw = kept("s_scales_raw", [P, K_PASSES * N], U8)
        s_scales = kept("s_scales", [P, SLOTS, K_PASSES * N // SLOTS], U8)
        ident = kept("ident", [P, P], BF16)
        bg_raw = kept("bg_raw", [GROUPS, PASS], BF16)
        weight_raw = kept("weight_raw", [GROUPS, PASS], BF16)
        bg_sorted = kept("bg_sorted", [P, PASS], BF16)
        weight_sorted = kept("weight_sorted", [P, PASS], BF16)
        bg_col = kept("bg_col", [P, SLOTS, GROUPS], F32)
        warm = kept("warm", [P, 1], F32)
        warm_out = kept("warm_out", [P, 1], F32)

        nc.vector.memset(s_scales_raw[:].bitcast(I32), 0)
        nc.vector.memset(a_scales[:].bitcast(I32), 0)
        nc.vector.memset(warm[:], 1.0)
        nc.vector.memset(bg_sorted[:], 0.0)
        nc.vector.memset(weight_sorted[:], 0.0)
        nc.scalar.activation(out=warm_out[:], in_=warm[:], func=FUNC.Ln)

        rows_raw = {}
        counts_raw = {}
        s_raw = {}
        a_words = {}

        def load_rows(key, rows):
            raw = rotating("rows_raw", "rows_raw_%s_%d" % key, [P, SLOTS, PASS], BF16, ROW_BUFS)
            nc.sync.dma_start(out=raw[:], in_=rows.rearrange("(p j) w -> p j w", j=SLOTS))
            rows_raw[key] = raw

        def load_prog(c):
            load_rows(("prog", c), prog[c * PASS:(c + 1) * PASS, :])

        def load_sig(g, c):
            load_rows((g, c), sig[c * PASS:(c + 1) * PASS, g * PASS:(g + 1) * PASS])

        def load_counts(u):
            half, g = divmod(u, GROUPS)
            raw = rotating("counts_raw", "counts_raw_%d" % u, [P, TILES, PASS], BF16, COUNT_BUFS)
            rows = counts_w[half * PASS:(half + 1) * PASS, g * PASS:(g + 1) * PASS]
            nc.sync.dma_start(out=raw[:], in_=rows.rearrange("(s p) n -> p s n", p=P))
            counts_raw[u] = raw

        def load_words(words, index, name):
            raw = kept("%s_%d" % (name, index), [P, K_PASSES, 2 * PASS], U8)
            part = words[:, :, index * 2 * PASS:(index + 1) * 2 * PASS].rearrange("c p n -> p c n")
            nc.sync.dma_start(out=raw[:].bitcast(I32), in_=part.bitcast(I32))
            return raw

        def load_s(g):
            s_raw[g] = load_words(sigq_words, g, "s_raw")

        def load_a(half):
            a_words[half] = load_words(abn_words, half, "a_words")

        def load_scales(plane, scales, quadrants):
            view = plane[:].rearrange("p (c n) -> p c n", c=K_PASSES)
            for quad in quadrants:
                nc.sync.dma_start(
                    out=view[32 * quad:32 * quad + 4, :, :].bitcast(I32),
                    in_=scales[:, 4 * quad:4 * quad + 4, :].rearrange("c r n -> r c n").bitcast(I32),
                )

        nc.gpsimd.dma_start(out=bg_raw[:], in_=bg.rearrange("(g n) -> g n", g=GROUPS))
        nc.gpsimd.dma_start(out=weight_raw[:], in_=gene_w.rearrange("(g n) -> g n", g=GROUPS))
        make_identity(nc, ident[:])

        load_s(0)
        load_a(0)
        load_scales(s_scales_raw, sigq_scales, range(QUADRANTS))
        load_scales(a_scales, abn_scales, range(1))
        load_prog(0)
        load_scales(a_scales, abn_scales, range(1, QUADRANTS))
        load_s(1)
        load_prog(1)
        load_sig(0, 0)
        load_counts(0)
        load_s(2)
        load_sig(0, 1)
        load_counts(1)
        load_sig(1, 0)
        load_s(3)
        load_sig(1, 1)
        load_counts(2)
        load_a(1)
        load_sig(2, 0)
        load_counts(3)
        load_sig(2, 1)
        load_counts(4)
        load_counts(5)

        s_words = {}
        grouped = {}
        codes = {}
        counts_sorted = {}
        counts_t = {}
        mu = {}
        inverse = {}
        ratio = {}
        res_grouped = {}
        proj_grouped = {}
        proj_bank = {}
        out_bank = {}

        def vector_columns(raw, sorted_rows, tag):
            nc.scalar.copy(
                out=sorted_rows[:GROUPS, :].rearrange("p (t q r) -> p t q r", t=SLOTS, r=RUN),
                in_=raw[:].rearrange("p (q t r) -> p t q r", t=SLOTS, r=RUN),
            )
            dst = bank(tag, "columns_" + tag, [P, SLOTS, P], BF16)
            for t in range(SLOTS):
                nc.tensor.transpose(dst[:, t, :], sorted_rows[:, t * P:(t + 1) * P], ident[:])
            return dst

        def sort_s(g):
            dst = kept("s_words_%d" % g, [P, SLOTS, K_PASSES * 2 * P], U8)
            src = s_raw[g][:].rearrange("p c n -> p (c n)").bitcast(I32)
            nc.vector.tensor_copy(
                out=dst[:].bitcast(I32).rearrange("p t (x w) -> p t x w", w=4),
                in_=src.rearrange("p (x t w) -> p t x w", t=SLOTS, w=4),
            )
            s_words[g] = dst

        def sort_s_scales():
            nc.vector.tensor_copy(
                out=s_scales[:].bitcast(I32).rearrange("p t (x w) -> p t x w", w=2),
                in_=s_scales_raw[:].bitcast(I32).rearrange("p (x t w) -> p t x w", t=SLOTS, w=2),
            )

        def interleave_prog(c):
            key = ("prog", c)
            dst = rotating("grouped", "grouped_prog_%d" % c, [P, PASS * SLOTS], BF16)
            nc.vector.tensor_copy(
                out=dst[:].rearrange("p (x i j) -> p x j i", i=4, j=SLOTS),
                in_=rows_raw[key][:].rearrange("p j (x i) -> p x j i", i=4),
            )
            grouped[key] = dst

        def interleave_sig(g, c, engine, timed):
            name = "grouped_%d_%d" % (g, c)
            shape = [P, PASS * SLOTS]
            dst = released(name, shape) if timed else rotating("grouped", name, shape, BF16)
            raw = rows_raw[(g, c)]
            if engine == GPSIMD:
                copy_on(
                    engine,
                    dst[:].rearrange("p (t q r j) -> p q t r j", t=SLOTS, r=RUN, j=SLOTS),
                    raw[:].rearrange("p j (q t r) -> p q t r j", t=SLOTS, r=RUN),
                )
            else:
                dst_view = dst[:].rearrange("p (t q a i j) -> p a q t j i", t=SLOTS, a=2, i=4, j=SLOTS)
                src_view = raw[:].rearrange("p j (q t a i) -> p a q t j i", t=SLOTS, a=2, i=4)
                for a in range(2):
                    copy_on(engine, dst_view[:, a], src_view[:, a])
            grouped[(g, c)] = dst

        def quantize(key, src, start=0, stop=PASS):
            if key not in codes:
                name = "%s_%d" % key
                codes[key] = (kept("codes_" + name, [P, PASS], U32), kept("scales_" + name, [P, PASS], U8))
            words, scales = codes[key]
            nc.vector.quantize_mx(
                out=words[:, start:stop].bitcast(FP8X4),
                scales=scales[:, start:stop],
                in_=src[:, start * SLOTS:stop * SLOTS],
            )

        def quantize_rows(key):
            quantize(key, grouped[key])

        def quantize_res(u, start=0, stop=PASS):
            quantize(("res", u), res_grouped[u], start, stop)

        def quantize_proj(g):
            quantize(("proj", g), proj_grouped[g])

        def sort_counts(u, engine):
            name = "counts_sorted_%d" % u
            shape = [P, SLOTS, PASS]
            dst = released(name, shape) if engine == GPSIMD else rotating("counts_sorted", name, shape, BF16)
            src = counts_raw[u][:].rearrange("p s n -> p (s n)")
            copy_on(
                engine,
                dst[:].rearrange("p t (x r) -> p t x r", r=RUN),
                src.rearrange("p (x t r) -> p t x r", t=SLOTS, r=RUN),
            )
            counts_sorted[u] = dst

        def transpose_counts(u):
            for piece in range(2):
                dst = bank("counts_t%d" % piece, "counts_t_%d_%d" % (u, piece), [P, SLOTS, PIECE], BF16)
                for t in range(SLOTS):
                    for s in range(PIECE // P):
                        col = piece * PIECE + s * P
                        nc.tensor.transpose(dst[:, t, s * P:(s + 1) * P], counts_sorted[u][:, t, col:col + P], ident[:])
                counts_t[(u, piece)] = dst

        def mu_matmul(n):
            u, t = divmod(n, SLOTS)
            half, g = divmod(u, GROUPS)
            dst = bank("mu%d" % (n % MU_BANKS), "mu_%d" % n, [P, PASS], F32)
            for c in range(K_PASSES):
                s_col = (c * GROUPS + g) * P
                a_col = c * M + half * PASS
                nc.tensor.matmul_mx(
                    out=dst[:],
                    lhsT=s_words[g][:, t, c * 2 * P:(c + 1) * 2 * P].bitcast(FP4X4),
                    lhsT_scale=s_scales[:, t, s_col:s_col + P],
                    rhs=a_words[half][:, c, :].bitcast(FP4X4),
                    rhs_scale=a_scales[:, a_col:a_col + PASS],
                    start=(c == 0),
                    stop=(c == K_PASSES - 1),
                )
            mu[n] = dst

        def log_rate(u, refills=SLOTS):
            g = u % GROUPS
            dst = rotating("inverse", "inverse_%d" % u, [P, SLOTS, PASS], F32, INVERSE_BUFS)
            inverse[u] = dst
            for t in range(SLOTS):
                n = u * SLOTS + t
                nc.scalar.activation(out=dst[:, t, :], in_=mu[n][:], func=FUNC.Ln, bias=bg_col[:, t, g:g + 1])
                if t < refills:
                    mu_matmul(n + MU_BANKS)

        def inverse_rate(u):
            for piece in range(2):
                part = inverse[u][:, :, piece * PIECE:(piece + 1) * PIECE]
                nc.scalar.activation(out=part, in_=part, func=FUNC.Exp, scale=-1.0)

        def multiply(u, piece):
            dst = rotating("ratio", "ratio_%d_%d" % (u, piece), [P, SLOTS, PIECE], F32)
            nc.vector.tensor_tensor(
                out=dst[:],
                in0=inverse[u][:, :, piece * PIECE:(piece + 1) * PIECE],
                in1=counts_t[(u, piece)][:],
                op=ALU.mult,
            )
            ratio[(u, piece)] = dst

        def subtract(u, piece, lo=0, hi=PIECE):
            g = u % GROUPS
            if u not in res_grouped:
                res_grouped[u] = rotating("res_grouped", "res_grouped_%d" % u, [P, PASS * SLOTS], BF16)
            part = res_grouped[u][:, (piece * PIECE + lo) * SLOTS:(piece * PIECE + hi) * SLOTS]
            weights = weight_t[:, :, g:g + 1].rearrange("p t (x i) -> p x t i", x=1)
            nc.vector.tensor_tensor(
                out=part.rearrange("p (x i t) -> p x t i", i=2, t=SLOTS),
                in0=ratio[(u, piece)][:, :, lo:hi].rearrange("p t (x i) -> p x t i", i=2),
                in1=weights.to_broadcast([P, (hi - lo) // 2, SLOTS, 2]),
                op=ALU.subtract,
            )

        def residual(u):
            multiply(u, 0)
            multiply(u, 1)
            subtract(u, 0)
            subtract(u, 1)

        def proj_matmuls(g, first, tags=("acc0", "acc1")):
            for b, tag in zip((first, first + 1), tags):
                dst = bank(tag, "proj_%d_%d" % (g, b), [P, SLOTS, P], F32)
                programs = slice(b * P, (b + 1) * P)
                for t in range(SLOTS):
                    genes = slice(t * P, (t + 1) * P)
                    for c in range(K_PASSES):
                        nc.tensor.matmul_mx(
                            out=dst[:, t, :],
                            lhsT=codes[(g, c)][0][:, genes].bitcast(FP8X4),
                            lhsT_scale=codes[(g, c)][1][:, genes],
                            rhs=codes[("prog", c)][0][:, programs].bitcast(FP8X4),
                            rhs_scale=codes[("prog", c)][1][:, programs],
                            start=(c == 0),
                            stop=(c == K_PASSES - 1),
                        )
                proj_bank[(g, b)] = dst

        def proj_copies(g, first, engine):
            if first == 0:
                proj_grouped[g] = rotating("proj_grouped", "proj_grouped_%d" % g, [P, R * SLOTS], BF16)
            for b in (first, first + 1):
                part = proj_grouped[g][:, b * P * SLOTS:(b + 1) * P * SLOTS]
                copy_on(
                    engine,
                    part.rearrange("p (r t) -> p r t", t=SLOTS),
                    proj_bank[(g, b)][:].rearrange("p t r -> p r t"),
                )

        out_tags = ["mu0", "acc0", "acc1", "mu1", "mu2"]

        def out_matmul(m, g):
            half, s = divmod(m, TILES)
            if g == 0:
                out_bank[m] = bank(out_tags[m % len(out_tags)], "out_%d" % m, [P, R], F32)
            spots = slice(s * P, (s + 1) * P)
            words, scales = codes[("res", half * GROUPS + g)]
            nc.tensor.matmul_mx(
                out=out_bank[m][:],
                lhsT=words[:, spots].bitcast(FP8X4),
                lhsT_scale=scales[:, spots],
                rhs=codes[("proj", g)][0][:].bitcast(FP8X4),
                rhs_scale=codes[("proj", g)][1][:],
                start=(g == 0),
                stop=(g == GROUPS - 1),
            )

        def out_store(m, engine):
            result = rotating("result", "result_%d" % m, [P, R], F32, RESULT_BUFS)
            copy_on(engine, result[:], out_bank[m][:])
            nc.sync.dma_start(out=out[m * P:(m + 1) * P, :], in_=result[:])


        bg_t = vector_columns(bg_raw, bg_sorted, "acc0")
        nc.scalar.copy(out=bg_col[:], in_=bg_t[:, :, :GROUPS])
        weight_t = vector_columns(weight_raw, weight_sorted, "weights")
        sort_s(0)
        sort_s_scales()
        for n in range(MU_BANKS):
            mu_matmul(n)
        interleave_prog(0)
        sort_s(1)
        log_rate(0)
        quantize_rows(("prog", 0))
        interleave_prog(1)
        load_sig(3, 0)
        load_sig(3, 1)
        interleave_sig(0, 0, VECTOR, timed=False)
        quantize_rows(("prog", 1))
        sort_counts(0, VECTOR)
        load_counts(6)
        log_rate(1, refills=1)
        transpose_counts(0)
        sort_s(2)
        for n in range(2 * SLOTS, 2 * SLOTS + MU_BANKS):
            mu_matmul(n)
        quantize_rows((0, 0))
        interleave_sig(0, 1, VECTOR, timed=True)
        sort_counts(1, VECTOR)
        load_counts(7)
        sort_s(3)
        quantize_rows((0, 1))
        inverse_rate(0)
        inverse_rate(1)
        proj_matmuls(0, 0)

        interleave_sig(1, 0, GPSIMD, timed=True)
        interleave_sig(1, 1, GPSIMD, timed=False)
        multiply(0, 0)
        multiply(0, 1)
        transpose_counts(1)
        proj_copies(0, 0, VECTOR)
        proj_matmuls(0, 2)
        subtract(0, 0)
        subtract(0, 1)
        proj_copies(0, 2, VECTOR)
        log_rate(2)
        sort_counts(2, VECTOR)
        quantize_res(0)
        quantize_rows((1, 1))
        quantize_rows((1, 0))

        interleave_sig(2, 0, GPSIMD, timed=True)
        log_rate(3)
        residual(1)
        log_rate(4)
        transpose_counts(2)
        proj_matmuls(1, 0)
        quantize_proj(0)
        quantize_res(1)
        sort_counts(3, VECTOR)
        quantize_rows((2, 0))
        inverse_rate(2)

        interleave_sig(2, 1, GPSIMD, timed=True)
        residual(2)
        transpose_counts(3)
        proj_copies(1, 0, SCALAR)
        proj_matmuls(1, 2)
        inverse_rate(3)
        inverse_rate(4)
        proj_copies(1, 2, SCALAR)
        sort_counts(4, VECTOR)
        quantize_res(2)
        quantize_rows((2, 1))
        proj_matmuls(2, 0)

        interleave_sig(3, 0, GPSIMD, timed=True)
        residual(3)
        log_rate(5)
        transpose_counts(4)
        proj_copies(2, 0, SCALAR)
        log_rate(6)
        sort_counts(5, VECTOR)
        quantize_proj(1)
        quantize_res(3)
        quantize_rows((3, 0))

        interleave_sig(3, 1, GPSIMD, timed=True)
        residual(4)
        log_rate(7, refills=1)
        transpose_counts(5)
        proj_matmuls(2, 2, ("mu2", "mu0"))
        inverse_rate(5)
        sort_counts(6, VECTOR)
        quantize_res(4)
        quantize_rows((3, 1))
        proj_matmuls(3, 0)

        sort_counts(7, GPSIMD)
        residual(5)
        transpose_counts(6)
        proj_copies(2, 2, SCALAR)
        proj_matmuls(3, 2, ("mu1", "mu2"))
        inverse_rate(6)
        proj_copies(3, 0, SCALAR)
        quantize_proj(2)
        quantize_res(5)
        proj_copies(3, 2, SCALAR)
        inverse_rate(7)

        multiply(6, 0)
        multiply(6, 1)
        quantize_proj(3)
        for g in range(GROUPS):
            for m in range(TILES):
                out_matmul(m, g)
            if g == GROUPS // 2 - 1:
                transpose_counts(7)
        subtract(6, 0)
        subtract(6, 1)

        last = UNITS - 1
        multiply(last, 0)
        quantize_res(last - 1)
        for m in range(TILES):
            out_matmul(TILES + m, 0)
            out_matmul(TILES + m, 1)
            out_store(m, SCALAR)
        for m in range(TILES):
            out_matmul(TILES + m, 2)
        subtract(last, 0)
        multiply(last, 1)
        quantize_res(last, 0, PIECE)
        out_matmul(TILES, GROUPS - 1)
        out_matmul(TILES + 1, GROUPS - 1)
        subtract(last, 1, 0, P)
        subtract(last, 1, P, PIECE)
        out_store(TILES, SCALAR)
        out_store(TILES + 1, SCALAR)
        quantize_res(last, PIECE, PIECE + P)
        out_matmul(TILES + 2, GROUPS - 1)
        quantize_res(last, PIECE + P, PASS)
        out_matmul(TILES + 3, GROUPS - 1)
        out_store(TILES + 2, SCALAR)
        out_store(TILES + 3, VECTOR)
